import numpy as np
import ml_dtypes


def mxq(x, axis, fmt="e4m3"):
    dtype, down = {"e4m3": (ml_dtypes.float8_e4m3fn, 7), "e5m2": (ml_dtypes.float8_e5m2, 14)}[fmt]
    v = np.moveaxis(np.asarray(x, np.float32).astype(ml_dtypes.bfloat16).astype(np.float64), axis, -1)
    blocks = v.reshape(v.shape[:-1] + (-1, 32))
    amax = np.abs(blocks).max(-1, keepdims=True)
    byte = np.maximum(np.where(amax > 0, np.frexp(amax)[1] - 1 + 127, 0) - down, 1)
    scale = np.exp2(byte - 127.0)
    codes = (blocks / scale).astype(np.float32).astype(dtype).astype(np.float64)
    return np.moveaxis((codes * scale).reshape(v.shape), -1, axis)


WIDE = False


def mx_kscale(k):
    if not WIDE:
        return np.ones(k)
    levels = np.array([10, -10, 5, -5, 0])
    if k % 512:
        return np.exp2(np.random.permutation(np.resize(levels, k // 32))).repeat(32)
    a = np.empty((k // 512, 16))
    for p in range(k // 512):
        a[p, :8] = np.random.permutation(np.resize(levels, 8))
        for g in range(8):
            far = levels[np.abs(levels - a[p, g]) >= 10]
            a[p, g + 8] = far[np.random.randint(len(far))]
    return np.exp2(a.ravel()).repeat(32)


BF16 = ml_dtypes.bfloat16


def bf(x):
    return np.asarray(x, np.float32).astype(BF16)


def f64(x):
    return np.asarray(x).astype(np.float64)


E2M1 = np.array([0.0, 0.5, 1.0, 1.5, 2.0, 3.0, 4.0, 6.0, -0.0, -0.5, -1.0, -1.5, -2.0, -3.0, -4.0, -6.0])


def pack_weight(w, fmt):
    k, n = w.shape
    w = f64(bf(w)).reshape(k // 32, 32, n)
    amax = np.abs(w).max(1)
    if fmt == "e4m3":
        byte = np.frexp(amax)[1] - 1 + 127 - 7
    else:
        mant, ex = np.frexp(amax / 6.0)
        byte = np.where(mant > 0.5, ex, ex - 1) + 127
    byte = np.clip(np.where(amax > 0, byte, 1), 1, 254)
    scaled = (w * np.exp2(127.0 - byte)[:, None, :]).reshape(k, n).astype(np.float32)
    by_word = np.ascontiguousarray(scaled.reshape(k // 512, 128, 4, n).transpose(0, 1, 3, 2))
    if fmt == "e4m3":
        words = by_word.astype(ml_dtypes.float8_e4m3fn).view(np.uint8)
    else:
        c = by_word.astype(ml_dtypes.float4_e2m1fn).view(np.uint8) & 0xF
        words = c[..., 0::2] | (c[..., 1::2] << 4)
    return np.ascontiguousarray(words), np.ascontiguousarray(byte.astype(np.uint8).reshape(k // 512, 16, n))


def unpack_weight(words, scales, fmt):
    g, p, n, _ = words.shape
    if fmt == "e4m3":
        vals = np.ascontiguousarray(words).view(ml_dtypes.float8_e4m3fn).astype(np.float64)
    else:
        nib = np.empty((g, p, n, 4), np.uint8)
        nib[..., 0::2] = words & 0xF
        nib[..., 1::2] = words >> 4
        vals = E2M1[nib]
    vals = vals * np.repeat(np.exp2(scales.astype(np.float64) - 127.0), 8, axis=1)[..., None]
    return vals.transpose(0, 1, 3, 2).reshape(g * 512, n)
def pack4(w):
    words, scales = pack_weight(w, "e2m1")
    return words.reshape(words.shape[0], 128, -1), scales


def unpack4(words, scales):
    return unpack_weight(words.reshape(words.shape[0], 128, -1, 2), scales, "e2m1")


E4M3FN = np.array([(-1.0 if i & 128 else 1.0) * ((1.0 + (i & 7) / 8.0) * 2.0 ** (((i >> 3) & 15) - 7) if i & 120 else (i & 7) * 2.0 ** -9) for i in range(256)])


def e4m3fn_bytes(y):
    return np.clip(np.asarray(y, np.float64), -448.0, 448.0).astype(np.float32).astype(ml_dtypes.float8_e4m3fn).view(np.uint8)


def e4m3fn_values(b):
    return E4M3FN[b]


B, D, K, M = 2048, 1024, 512, 512


def stable_softmax(z):
    e = np.exp(z - np.max(z, axis=-1, keepdims=True))
    return e / np.sum(e, axis=-1, keepdims=True)


def stable_logsumexp(z):
    top = np.max(z, axis=-1, keepdims=True)
    return top + np.log(np.sum(np.exp(z - top), axis=-1, keepdims=True))


def draw0():
    s, r = mx_kscale(D), mx_kscale(K)
    x = bf(np.random.standard_normal((B, D)) * s[None, :])
    c1_words, c1_scales = pack4((np.random.standard_normal((K, D)) / np.sqrt(D) / s[None, :]).T)
    v1_words, v1_scales = pack4((0.5 * np.random.standard_normal((K, D)) * s[None, :] / r[:, None]).T)
    c2_words, c2_scales = pack4((np.random.standard_normal((M, D)) / np.sqrt(D) / s[None, :]).T)
    return {
        "x": x,
        "c1_words": c1_words,
        "c1_scales": c1_scales,
        "v1_words": v1_words,
        "v1_scales": v1_scales,
        "c2_words": c2_words,
        "c2_scales": c2_scales,
        "g": bf(4.0 * np.random.standard_normal(K) * r),
        "b1": bf(0.5 * np.random.standard_normal(K)),
        "b2": bf(0.5 * np.random.standard_normal(M)),
    }


def core(x, c1_words, c1_scales, v1_words, v1_scales, c2_words, c2_scales, g, b1, b2):
    xq = mxq(f64(x), 1, "e4m3")
    c2q = unpack4(c2_words, c2_scales).T
    s1 = xq @ unpack4(c1_words, c1_scales)
    s2 = xq @ c2q.T
    cross = unpack4(v1_words, v1_scales).T @ c2q.T
    p1 = stable_softmax(2.0 * s1 + f64(b1)[None, :])
    a = p1 * f64(g)[None, :]
    t = mxq(a, 1, "e4m3") @ mxq(cross, 0, "e4m3")
    l2 = s2 - t + f64(b2)[None, :]
    log_m = np.log(c2q.shape[0])
    return l2 - stable_logsumexp(l2) + log_m


def setup_inputs():
    drawn = draw0()
    full = np.asarray(drawn['x']).astype(np.float64)
    scale = (np.abs(full).reshape(2048, 8, 128).max(axis=(2,)) / 448.0).astype(np.float32)
    given = {}
    for key, value in drawn.items():
        if key == 'x':
            given['x_bytes'] = e4m3fn_bytes(full / np.repeat(scale.astype(np.float64), 128, axis=1))
            given['x_scale'] = scale
        else:
            given[key] = value
    return given


def reference(x_bytes, x_scale, c1_words, c1_scales, v1_words, v1_scales, c2_words, c2_scales, g, b1, b2):
    return core(e4m3fn_values(x_bytes) * np.repeat(x_scale.astype(np.float64), 128, axis=1), c1_words, c1_scales, v1_words, v1_scales, c2_words, c2_scales, g, b1, b2)

@@ -1,0 +1,454 @@
+import math
+from contextlib import ExitStack
+
+import concourse.mybir as mybir
+from concourse.masks import make_identity
+
+TOKENS, DIM, CODES = 2048, 1024, 512
+FLOPS = 2 * (2 * TOKENS * DIM * CODES + CODES * DIM * CODES + TOKENS * CODES * CODES)
+
+F32 = mybir.dt.float32
+BF16 = mybir.dt.bfloat16
+I32 = mybir.dt.int32
+U32 = mybir.dt.uint32
+U8 = mybir.dt.uint8
+FP8 = mybir.dt.float8_e4m3fn
+FP8X4 = mybir.dt.float8_e4m3fn_x4
+FP4X4 = mybir.dt.float4_e2m1fn_x4
+ALU = mybir.AluOpType
+ACT = mybir.ActivationFunctionType
+AX = mybir.AxisListType
+
+P = 128
+TILES = TOKENS // P
+PASSES = DIM // 512
+BLOCKS = DIM // 128
+CHUNKS = [(0, 1), (1, 3), (3, 6), (6, 10), (10, 14), (14, 16)]
+LOG_BATCHES = {4: 0, 10: 4, 13: 10, 16: 13}
+FINISH = "gggggggggggggvsg"
+ROOT = 256.0
+LOG_WAIT = 1
+VECTOR_BLOCKS = [5, 8, 0, 4, 0, 0, 0, 1, 0, 1, 0, 0, 0, 1, 0, 1]
+VECTOR_COPIES = [2, 1]
+CROSS_OUT = "vvss"
+CROSS_COPY = "ss"
+STEP = (
+    ("logits1", 0),
+    ("exp2", 3),
+    ("amplitude", 1),
+    ("turn_x", -2),
+    ("turn_a", 1),
+    ("min1", 0),
+    ("copy_a", 1),
+    ("logits2", 2),
+    ("score2", 1),
+    ("quant_x", -1),
+    ("quant_a", 1),
+    ("score1", -1),
+    ("exp1", 0),
+    ("min2", 2),
+    ("recon", 1),
+    ("recip1", 0),
+    ("widen", -3),
+    ("copy_x", -2),
+)
+CROSS = {(0, "copy_a"): (1,), (0, "quant_a"): (2,), (0, "recip1"): (3,), (1, "amplitude"): (4,), (1, "score1"): (5,)}
+
+
+def tile_softresidualsemanticids_d1p_kernel(
+    tc, x_bytes, x_scale, c1_words, c1_scales, v1_words, v1_scales, c2_words, c2_scales, g, b1, b2, out
+):
+    nc = tc.nc
+    x_view = x_bytes.rearrange("(p i) k -> p i k", i=TILES)
+    out_view = out.rearrange("(p i) m -> p i m", i=TILES)
+
+    with ExitStack() as ctx:
+        keep = ctx.enter_context(tc.tile_pool(name="keep", bufs=1))
+        work = ctx.enter_context(tc.tile_pool(name="work", bufs=3))
+        psum = ctx.enter_context(tc.psum_pool(name="psum", bufs=2))
+        ctx.enter_context(tc.manual_schedule())
+
+        scale_planes = {}
+        for name in ("c1", "v1", "c2"):
+            plane = keep.tile([P, PASSES, CODES], U8, name="scales_" + name, align_bytes=64)
+            nc.vector.memset(plane[:].rearrange("p g n -> p (g n)").bitcast(I32), 0)
+            scale_planes[name] = plane
+        ident = keep.tile([P, P], F32, name="ident")
+        make_identity(nc, ident[:])
+
+        words = {}
+
+        def load_words(name, source, queue=nc.gpsimd):
+            tile = keep.tile([P, PASSES, 2 * CODES], U8, name="words_" + name, align_bytes=64)
+            queue.dma_start(
+                out=tile[:].rearrange("p g n -> p (g n)").bitcast(I32).rearrange("p (g n) -> p g n", g=PASSES),
+                in_=source.bitcast(I32).rearrange("g p n -> p g n"),
+            )
+            words[name] = tile
+
+        def load_scales(name, source):
+            plane = scale_planes[name]
+            view = plane[:].rearrange("p g n -> p (g n)").bitcast(I32).rearrange("p (g n) -> p g n", g=PASSES)
+            rows = source.bitcast(I32).rearrange("g q n -> q g n")
+            for quad in range(4):
+                nc.sync.dma_start(out=view[32 * quad : 32 * quad + 4], in_=rows[4 * quad : 4 * quad + 4])
+
+        def load_row(name, source):
+            tile = keep.tile([P, CODES], BF16, name="row_" + name)
+            nc.gpsimd.dma_start(out=tile[:], in_=source.partition_broadcast(P))
+            return tile
+
+        x_tiles = {}
+
+        def load_x(chunk):
+            lo, hi = chunk
+            tile = keep.tile([P, hi - lo, DIM], U8, name="xbytes_" + str(lo), align_bytes=64)
+            nc.sync.dma_start(out=tile[:], in_=x_view[:, lo:hi, :])
+            for i in range(lo, hi):
+                x_tiles[i] = (tile, i - lo)
+
+        scale_cols = keep.tile([P, TILES * BLOCKS], F32, name="scale_cols")
+        nc.sync.dma_start(out=scale_cols[:], in_=x_scale.rearrange("(p i) j -> p (i j)", i=TILES))
+        load_x(CHUNKS[0])
+        load_scales("c1", c1_scales)
+        load_words("c1", c1_words, nc.sync)
+        load_x(CHUNKS[1])
+        row_b1 = load_row("b1", b1)
+        load_words("v1", v1_words)
+        load_words("c2", c2_words)
+        row_g = load_row("g", g)
+        row_b2 = load_row("b2", b2)
+        neg_g = keep.tile([P, CODES], BF16, name="neg_g")
+        nc.gpsimd.tensor_scalar(out=neg_g[:], in0=row_g[:], scalar1=-1.0, scalar2=0.0, op0=ALU.mult, op1=ALU.add)
+        load_scales("v1", v1_scales)
+        load_scales("c2", c2_scales)
+        for chunk in CHUNKS[2:]:
+            load_x(chunk)
+        warm = keep.tile([P, 1], F32, name="warm")
+        nc.vector.memset(warm[:], 0.0)
+        warm_out = keep.tile([P, 1], F32, name="warm_out")
+        nc.scalar.activation(out=warm_out[:], in_=warm[:], func=ACT.Exp)
+
+        root = keep.tile([P, 2, 6], F32, name="root")
+        nc.gpsimd.memset(root[:, 0, :], 1.0 / ROOT)
+        nc.gpsimd.memset(root[:, 1, :], -1.0 / ROOT)
+
+        s = {}
+        min2 = keep.tile([P, TILES], F32, name="min2")
+        sum2 = keep.tile([P, TILES], F32, name="sum2")
+
+        def mover(who):
+            return nc.vector.tensor_copy if who == "v" else nc.scalar.copy
+
+        def ok(i):
+            return 0 <= i < TILES
+
+        def widen(i):
+            if not ok(i):
+                return
+            vector_blocks = VECTOR_BLOCKS[i]
+            tile, slot = x_tiles[i]
+            xb = work.tile([P, DIM], BF16, name="xb")
+            for j in range(BLOCKS):
+                cols = slice(128 * j, 128 * j + 128)
+                src = tile[:, slot, cols].bitcast(FP8)
+                scale = scale_cols[:, BLOCKS * i + j : BLOCKS * i + j + 1]
+                if j < vector_blocks:
+                    nc.vector.tensor_scalar(out=xb[:, cols], in0=src, scalar1=scale, scalar2=None, op0=ALU.mult)
+                else:
+                    nc.scalar.activation(out=xb[:, cols], in_=src, func=ACT.Copy, scale=scale)
+            s["xb", i] = xb
+
+        def turn_x(i):
+            if not ok(i):
+                return
+            w = s.pop(("xb", i))[:].bitcast(F32)
+            xt = psum.tile([P, PASSES, 2, P], F32, name="xt")
+            for p in range(PASSES):
+                for u in range(2):
+                    nc.tensor.transpose(xt[:, p, u, :], w[:, 256 * p + u : 256 * (p + 1) : 2], ident[:])
+            s["xt", i] = xt
+
+        def copy_x(i):
+            if not ok(i):
+                return
+            engine = nc.vector.tensor_copy if i in VECTOR_COPIES else nc.scalar.copy
+            xt = s.pop(("xt", i))
+            xg = work.tile([P, PASSES * P * 4], BF16, name="xg", align_bytes=64)
+            dst = xg[:].bitcast(F32).rearrange("p (g r u) -> p g r u", g=PASSES, u=2)
+            engine(out=dst, in_=xt[:].rearrange("p g u r -> p g r u"))
+            s["xg", i] = xg
+
+        def quant_x(i):
+            if not ok(i):
+                return
+            xg = s.pop(("xg", i))
+            xc = work.tile([P, PASSES * P], U32, name="xc", align_bytes=64)
+            xs = work.tile([P, PASSES * P], U8, name="xs", align_bytes=64)
+            nc.vector.quantize_mx(out=xc[:].bitcast(FP8X4), scales=xs[:], in_=xg[:])
+            s["xq", i] = (xc, xs)
+
+        def x_passes(i, name, acc, last):
+            xc, xs = s["xq", i]
+            for p in range(PASSES):
+                cols = slice(P * p, P * p + P)
+                nc.tensor.matmul_mx(
+                    out=acc[:],
+                    lhsT=xc[:, cols].bitcast(FP8X4),
+                    lhsT_scale=xs[:, cols],
+                    rhs=words[name][:, p, :].bitcast(FP4X4),
+                    rhs_scale=scale_planes[name][:, p, :],
+                    start=(p == 0),
+                    stop=(last and p == PASSES - 1),
+                )
+
+        def score1(i):
+            if not ok(i):
+                return
+            acc = psum.tile([P, CODES], F32, name="acc1")
+            x_passes(i, "c1", acc, True)
+            s["acc1", i] = acc
+
+        def score2(i):
+            if not ok(i):
+                return
+            acc = psum.tile([P, CODES], F32, name="acc2")
+            x_passes(i, "c2", acc, False)
+            s["acc2", i] = acc
+
+        def recon(i):
+            if not ok(i):
+                return
+            ac, as_ = s.pop(("aq", i))
+            nc.tensor.matmul_mx(
+                out=s["acc2", i][:],
+                lhsT=ac[:].bitcast(FP8X4),
+                lhsT_scale=as_[:],
+                rhs=cross_codes[:].bitcast(FP8X4),
+                rhs_scale=cross_scales[:],
+                start=False,
+                stop=True,
+            )
+
+        def logits1(i):
+            if not ok(i):
+                return
+            z = work.tile([P, CODES], F32, name="z")
+            nc.vector.scalar_tensor_tensor(
+                out=z[:], in0=s.pop(("acc1", i))[:], scalar=-2.0, in1=row_b1[:], op0=ALU.mult, op1=ALU.subtract
+            )
+            s["z", i] = z
+
+        def min1(i):
+            if not ok(i):
+                return
+            m = work.tile([P, 1], F32, name="m1")
+            nc.vector.tensor_reduce(out=m[:], in_=s["z", i][:], axis=AX.X, op=ALU.min)
+            s["m1", i] = m
+
+        def exp1(i):
+            if not ok(i):
+                return
+            e = work.tile([P, CODES], F32, name="e")
+            total = work.tile([P, 1], F32, name="total")
+            nc.scalar.activation(
+                out=e[:], in_=s.pop(("z", i))[:], func=ACT.Exp, bias=s.pop(("m1", i))[:], scale=-1.0, accum_out=total[:]
+            )
+            s["e", i] = e
+            s["total", i] = total
+
+        def recip1(i):
+            if not ok(i):
+                return
+            r = work.tile([P, 1], F32, name="r")
+            nc.vector.reciprocal(out=r[:], in_=s.pop(("total", i))[:])
+            s["r", i] = r
+
+        def amplitude(i):
+            if not ok(i):
+                return
+            a = work.tile([P, CODES], BF16, name="a")
+            nc.vector.scalar_tensor_tensor(
+                out=a[:], in0=s.pop(("e", i))[:], scalar=s.pop(("r", i))[:], in1=neg_g[:], op0=ALU.mult, op1=ALU.mult
+            )
+            s["a", i] = a
+
+        def turn_a(i):
+            if not ok(i):
+                return
+            w = s.pop(("a", i))[:].bitcast(F32)
+            at = psum.tile([P, 2, P], F32, name="at")
+            for u in range(2):
+                nc.tensor.transpose(at[:, u, :], w[:, u:256:2], ident[:])
+            s["at", i] = at
+
+        def copy_a(i):
+            if not ok(i):
+                return
+            at = s.pop(("at", i))
+            ag = work.tile([P, P * 4], BF16, name="ag", align_bytes=64)
+            nc.scalar.copy(out=ag[:].bitcast(F32).rearrange("p (r u) -> p r u", u=2), in_=at[:].rearrange("p u r -> p r u"))
+            s["ag", i] = ag
+
+        def quant_a(i):
+            if not ok(i):
+                return
+            ac = work.tile([P, P], U32, name="ac", align_bytes=64)
+            as_ = work.tile([P, P], U8, name="as_", align_bytes=64)
+            nc.vector.quantize_mx(out=ac[:].bitcast(FP8X4), scales=as_[:], in_=s.pop(("ag", i))[:])
+            s["aq", i] = (ac, as_)
+
+        def logits2(i):
+            if not ok(i):
+                return
+            nl = keep.tile([P, CODES], F32, name="nl_" + str(i))
+            nc.vector.scalar_tensor_tensor(
+                out=nl[:], in0=s.pop(("acc2", i))[:], scalar=-1.0, in1=row_b2[:], op0=ALU.mult, op1=ALU.subtract
+            )
+            s["nl", i] = nl
+
+        def min2_of(i):
+            if not ok(i):
+                return
+            nc.vector.tensor_reduce(out=min2[:, i : i + 1], in_=s["nl", i][:], axis=AX.X, op=ALU.min)
+
+        def exp2(i):
+            if not ok(i):
+                return
+            if i - LOG_WAIT + 1 in LOG_BATCHES:
+                series_end(LOG_BATCHES[i - LOG_WAIT + 1], i - LOG_WAIT + 1)
+            spill = work.tile([P, CODES], BF16, name="spill")
+            nc.scalar.activation(
+                out=spill[:], in_=s["nl", i][:], func=ACT.Exp, bias=min2[:, i : i + 1], scale=-1.0,
+                accum_out=sum2[:, i : i + 1],
+            )
+            if i + 1 in LOG_BATCHES:
+                lo = LOG_BATCHES[i + 1]
+                if i + 1 == TILES:
+                    last_logs(lo, i + 1)
+                else:
+                    series_start(lo, i + 1)
+
+        def last_logs(lo, hi):
+            logs = keep.tile([P, hi - lo], F32, name="logs")
+            shift = keep.tile([P, hi - lo], F32, name="shift_" + str(lo))
+            nc.scalar.activation(out=logs[:], in_=sum2[:, lo:hi], func=ACT.Ln, scale=1.0 / CODES)
+            nc.vector.tensor_tensor(out=shift[:], in0=min2[:, lo:hi], in1=logs[:], op=ALU.subtract)
+            finish(lo, hi, shift)
+
+        def series_start(lo, hi):
+            n = hi - lo
+            total = sum2[:, lo:hi]
+            up = work.tile([P, n], F32, name="up")
+            nc.gpsimd.tensor_tensor(out=up[:], in0=total, in1=root[:, 0, 0:n], op=ALU.pow)
+            down = work.tile([P, n], F32, name="down")
+            nc.gpsimd.tensor_tensor(out=down[:], in0=total, in1=root[:, 1, 0:n], op=ALU.pow)
+            sinh2 = work.tile([P, n], F32, name="sinh2")
+            nc.gpsimd.tensor_tensor(out=sinh2[:], in0=up[:], in1=down[:], op=ALU.subtract)
+            s["log", lo] = sinh2
+
+        def series_end(lo, hi):
+            n = hi - lo
+            total = sum2[:, lo:hi]
+            sinh2 = s.pop(("log", lo))
+            shift = keep.tile([P, n], F32, name="shift_" + str(lo))
+            inv = work.tile([P, n], F32, name="inv")
+            nc.scalar.activation(out=inv[:], in_=sinh2[:], func=ACT.Exp, scale=-0.5 * ROOT)
+            ratio = work.tile([P, n], F32, name="ratio")
+            nc.gpsimd.tensor_tensor(out=ratio[:], in0=total, in1=inv[:], op=ALU.mult)
+            guess = work.tile([P, n], F32, name="guess")
+            nc.gpsimd.tensor_scalar(
+                out=guess[:], in0=sinh2[:], scalar1=0.5 * ROOT, scalar2=-math.log(CODES), op0=ALU.mult, op1=ALU.add
+            )
+            delta = work.tile([P, n], F32, name="delta")
+            nc.gpsimd.tensor_scalar(out=delta[:], in0=ratio[:], scalar1=1.0, scalar2=-1.0, op0=ALU.mult, op1=ALU.add)
+            slope = work.tile([P, n], F32, name="slope")
+            nc.gpsimd.tensor_scalar(out=slope[:], in0=ratio[:], scalar1=-0.5, scalar2=1.5, op0=ALU.mult, op1=ALU.add)
+            prod = work.tile([P, n], F32, name="prod")
+            nc.gpsimd.tensor_tensor(out=prod[:], in0=slope[:], in1=delta[:], op=ALU.mult)
+            log = work.tile([P, n], F32, name="log")
+            nc.gpsimd.tensor_tensor(out=log[:], in0=prod[:], in1=guess[:], op=ALU.add)
+            nc.gpsimd.tensor_tensor(out=shift[:], in0=min2[:, lo:hi], in1=log[:], op=ALU.subtract)
+            finish(lo, hi, shift)
+
+        def finish(lo, hi, shift):
+            res = work.tile([P, 6, CODES], F32, name="res", bufs=2)
+            for i in range(lo, hi):
+                who = FINISH[i]
+                src, dst, sh = s.pop(("nl", i))[:], res[:, i - lo, :], shift[:, i - lo : i - lo + 1]
+                if who == "s":
+                    nc.scalar.activation(out=dst, in_=src, func=ACT.Identity, bias=sh, scale=-1.0)
+                else:
+                    eng = nc.vector if who == "v" else nc.gpsimd
+                    eng.tensor_scalar(out=dst, in0=src, scalar1=-1.0, scalar2=sh, op0=ALU.mult, op1=ALU.add)
+            nc.sync.dma_start(out=out_view[:, lo:hi, :], in_=res[:, 0 : hi - lo, :])
+
+        cross_rows = keep.tile([P, 4, CODES], BF16, name="cross_rows")
+        cross_grouped = keep.tile([P, 4 * CODES], BF16, name="cross_grouped", align_bytes=64)
+        cross_codes = keep.tile([P, CODES], U32, name="cross_codes", align_bytes=64)
+        cross_scales = keep.tile([P, CODES], U8, name="cross_scales", align_bytes=64)
+
+        def cross_mm(j):
+            acc = psum.tile([P, CODES], F32, name="acc2")
+            for p in range(PASSES):
+                nc.tensor.matmul_mx(
+                    out=acc[:],
+                    lhsT=words["c2"][:, p, 256 * j : 256 * j + 256].bitcast(FP4X4),
+                    lhsT_scale=scale_planes["c2"][:, p, P * j : P * j + P],
+                    rhs=words["v1"][:, p, :].bitcast(FP4X4),
+                    rhs_scale=scale_planes["v1"][:, p, :],
+                    start=(p == 0),
+                    stop=(p == PASSES - 1),
+                )
+            s["cross", j] = acc
+
+        def cross_out(j, engine):
+            engine(out=cross_rows[:, j, :], in_=s.pop(("cross", j))[:])
+
+        def cross_turn(h):
+            ct = psum.tile([P, 2, 2, P], F32, name="at")
+            for jj in range(2):
+                w = cross_rows[:, 2 * h + jj, :].bitcast(F32)
+                for u in range(2):
+                    nc.tensor.transpose(ct[:, jj, u, :], w[:, u:256:2], ident[:])
+            s["ct", h] = ct
+
+        def cross_copy(h, engine):
+            dst = cross_grouped[:].bitcast(F32).rearrange("p (h j m u) -> p h j m u", h=2, j=2, u=2)[:, h]
+            engine(out=dst, in_=s.pop(("ct", h))[:].rearrange("p j u m -> p j m u"))
+
+        def cross_quant():
+            nc.vector.quantize_mx(out=cross_codes[:].bitcast(FP8X4), scales=cross_scales[:], in_=cross_grouped[:])
+
+        def cross_1():
+            cross_mm(0)
+            cross_mm(1)
+
+        def cross_2():
+            cross_out(0, mover(CROSS_OUT[0]))
+            cross_out(1, mover(CROSS_OUT[1]))
+            cross_mm(2)
+            cross_mm(3)
+
+        def cross_3():
+            cross_out(2, mover(CROSS_OUT[2]))
+            cross_out(3, mover(CROSS_OUT[3]))
+            cross_turn(0)
+            cross_turn(1)
+
+        def cross_4():
+            cross_copy(0, mover(CROSS_COPY[0]))
+            cross_copy(1, mover(CROSS_COPY[1]))
+
+        pieces = {1: cross_1, 2: cross_2, 3: cross_3, 4: cross_4, 5: cross_quant}
+        ops = {
+            "widen": widen, "turn_x": turn_x, "copy_x": copy_x, "quant_x": quant_x, "score1": score1,
+            "logits1": logits1, "min1": min1, "exp1": exp1, "recip1": recip1, "amplitude": amplitude,
+            "turn_a": turn_a, "copy_a": copy_a, "quant_a": quant_a, "score2": score2, "recon": recon,
+            "logits2": logits2, "min2": min2_of, "exp2": exp2,
+        }
+        for k in range(-4, TILES + 6):
+            for name, lag in STEP:
+                ops[name](k - lag)
+                for piece in CROSS.get((k, name), ()):
+                    pieces[piece]()

@@ -24,35 +24,54 @@ TILES = TOKENS // P
 PASSES = DIM // 512
 BLOCKS = DIM // 128
 CHUNKS = [(0, 1), (1, 3), (3, 6), (6, 10), (10, 14), (14, 16)]
-LOG_BATCHES = {4: 0, 10: 4, 13: 10, 16: 13}
-FINISH = "gggggggggggggvsg"
+LOG_BATCHES = {7: 0, 11: 7, 16: 11}
+FINISH = "ssssvvvvvvvvvvvv"
+VECTOR_BLOCKS = [2, 5, 0, 2, 1, 5, 2, 1, 2, 0, 2, 0, 2, 0, 0, 0]
+VECTOR_COPIES = [0, 1]
+STORE = 1
 ROOT = 256.0
 LOG_WAIT = 1
-VECTOR_BLOCKS = [5, 8, 0, 4, 0, 0, 0, 1, 0, 1, 0, 0, 0, 1, 0, 1]
-VECTOR_COPIES = [2, 1]
+FIN_WAIT = 2
+AMP = "vvvvvvvvvvvvvvvv"
 CROSS_OUT = "vvss"
-CROSS_COPY = "ss"
+CROSS_COPY = "vv"
+GROUPS = [(0, 1), (1, 3), (3, 5), (5, 7), (7, 9), (9, 11), (11, 13), (13, 15), (15, 16)]
 STEP = (
-    ("logits1", 0),
-    ("exp2", 3),
-    ("amplitude", 1),
-    ("turn_x", -2),
-    ("turn_a", 1),
-    ("min1", 0),
-    ("copy_a", 1),
-    ("logits2", 2),
-    ("score2", 1),
-    ("quant_x", -1),
-    ("quant_a", 1),
-    ("score1", -1),
-    ("exp1", 0),
-    ("min2", 2),
-    ("recon", 1),
-    ("recip1", 0),
-    ("widen", -3),
-    ("copy_x", -2),
+    ("logits1", 0, 0),
+    ("turn_x", -2, 0),
+    ("widen", -3, 0),
+    ("logits1", 0, 1),
+    ("amplitude", 1, 0),
+    ("amplitude", 1, 1),
+    ("turn_x", -2, 1),
+    ("finish", 1, 0),
+    ("min1", 0, -1),
+    ("exp2", 3, 0),
+    ("logits2", 2, 0),
+    ("quant_x", -1, -1),
+    ("turn_a", 1, -1),
+    ("exp2", 3, 1),
+    ("copy_a", 1, -1),
+    ("score2", 1, 0),
+    ("logits2", 2, 1),
+    ("score1", -1, 0),
+    ("exp1", 0, 0),
+    ("score1", -1, 1),
+    ("quant_a", 1, -1),
+    ("recon", 1, 0),
+    ("exp1", 0, 1),
+    ("finish", -1, 2),
+    ("min2", 2, -1),
+    ("widen", -3, 1),
+    ("copy_x", -2, 0),
+    ("finish", 27, 1),
+    ("score2", 1, 1),
+    ("recip1", 0, -1),
+    ("copy_x", -2, 1),
+    ("finish", -15, 3),
+    ("recon", 1, 1),
 )
-CROSS = {(0, "copy_a"): (1,), (0, "quant_a"): (2,), (0, "recip1"): (3,), (1, "amplitude"): (4,), (1, "score1"): (5,)}
+CROSS = {(-1, "widen", 0): (1,), (-1, "finish", 2): (2,), (0, "turn_x", 0): (3,), (0, "copy_a", -1): (4,), (1, "copy_a", -1): (5,)}
 
 
 def tile_softresidualsemanticids_d1p_kernel(
@@ -93,9 +112,9 @@ def tile_softresidualsemanticids_d1p_kernel(
             for quad in range(4):
                 nc.sync.dma_start(out=view[32 * quad : 32 * quad + 4], in_=rows[4 * quad : 4 * quad + 4])
 
-        def load_row(name, source):
+        def load_row(name, source, queue=nc.gpsimd):
             tile = keep.tile([P, CODES], BF16, name="row_" + name)
-            nc.gpsimd.dma_start(out=tile[:], in_=source.partition_broadcast(P))
+            queue.dma_start(out=tile[:], in_=source.partition_broadcast(P))
             return tile
 
         x_tiles = {}
@@ -107,13 +126,13 @@ def tile_softresidualsemanticids_d1p_kernel(
             for i in range(lo, hi):
                 x_tiles[i] = (tile, i - lo)
 
+        load_x(CHUNKS[0])
         scale_cols = keep.tile([P, TILES * BLOCKS], F32, name="scale_cols")
         nc.sync.dma_start(out=scale_cols[:], in_=x_scale.rearrange("(p i) j -> p (i j)", i=TILES))
-        load_x(CHUNKS[0])
         load_scales("c1", c1_scales)
         load_words("c1", c1_words, nc.sync)
         load_x(CHUNKS[1])
-        row_b1 = load_row("b1", b1)
+        row_b1 = load_row("b1", b1, nc.sync)
         load_words("v1", v1_words)
         load_words("c2", c2_words)
         row_g = load_row("g", g)
@@ -129,7 +148,7 @@ def tile_softresidualsemanticids_d1p_kernel(
         warm_out = keep.tile([P, 1], F32, name="warm_out")
         nc.scalar.activation(out=warm_out[:], in_=warm[:], func=ACT.Exp)
 
-        root = keep.tile([P, 2, 6], F32, name="root")
+        root = keep.tile([P, 2, TILES], F32, name="root")
         nc.gpsimd.memset(root[:, 0, :], 1.0 / ROOT)
         nc.gpsimd.memset(root[:, 1, :], -1.0 / ROOT)
 
@@ -140,58 +159,57 @@ def tile_softresidualsemanticids_d1p_kernel(
         def mover(who):
             return nc.vector.tensor_copy if who == "v" else nc.scalar.copy
 
-        def ok(i):
-            return 0 <= i < TILES
+        def ok(j):
+            return 0 <= j < len(GROUPS)
 
-        def widen(i):
-            if not ok(i):
-                return
-            vector_blocks = VECTOR_BLOCKS[i]
+        def tiles(j):
+            return range(GROUPS[j][0], GROUPS[j][1])
+
+        def span(j):
+            return GROUPS[j][1] - GROUPS[j][0]
+
+        def widen(j, q):
+            if q == 0:
+                s["xb", j] = work.tile([P, 2, DIM], BF16, name="xb")
+            i = GROUPS[j][0] + q
             tile, slot = x_tiles[i]
-            xb = work.tile([P, DIM], BF16, name="xb")
-            for j in range(BLOCKS):
-                cols = slice(128 * j, 128 * j + 128)
+            xb = s["xb", j]
+            for b in range(BLOCKS):
+                cols = slice(128 * b, 128 * b + 128)
                 src = tile[:, slot, cols].bitcast(FP8)
-                scale = scale_cols[:, BLOCKS * i + j : BLOCKS * i + j + 1]
-                if j < vector_blocks:
-                    nc.vector.tensor_scalar(out=xb[:, cols], in0=src, scalar1=scale, scalar2=None, op0=ALU.mult)
+                scale = scale_cols[:, BLOCKS * i + b : BLOCKS * i + b + 1]
+                if b < VECTOR_BLOCKS[i]:
+                    nc.vector.tensor_scalar(out=xb[:, q, cols], in0=src, scalar1=scale, scalar2=None, op0=ALU.mult)
                 else:
-                    nc.scalar.activation(out=xb[:, cols], in_=src, func=ACT.Copy, scale=scale)
-            s["xb", i] = xb
+                    nc.scalar.activation(out=xb[:, q, cols], in_=src, func=ACT.Copy, scale=scale)
 
-        def turn_x(i):
-            if not ok(i):
-                return
-            w = s.pop(("xb", i))[:].bitcast(F32)
+        def turn_x(j, q):
+            w = s["xb", j][:, q, :].bitcast(F32)
             xt = psum.tile([P, PASSES, 2, P], F32, name="xt")
             for p in range(PASSES):
                 for u in range(2):
                     nc.tensor.transpose(xt[:, p, u, :], w[:, 256 * p + u : 256 * (p + 1) : 2], ident[:])
-            s["xt", i] = xt
+            s["xt", j, q] = xt
 
-        def copy_x(i):
-            if not ok(i):
-                return
-            engine = nc.vector.tensor_copy if i in VECTOR_COPIES else nc.scalar.copy
-            xt = s.pop(("xt", i))
-            xg = work.tile([P, PASSES * P * 4], BF16, name="xg", align_bytes=64)
-            dst = xg[:].bitcast(F32).rearrange("p (g r u) -> p g r u", g=PASSES, u=2)
-            engine(out=dst, in_=xt[:].rearrange("p g u r -> p g r u"))
-            s["xg", i] = xg
+        def copy_x(j, q):
+            if q == 0:
+                s["xg", j] = work.tile([P, 2 * PASSES * P * 4], BF16, name="xg", align_bytes=64)
+            engine = nc.vector.tensor_copy if GROUPS[j][0] + q in VECTOR_COPIES else nc.scalar.copy
+            dst = s["xg", j][:, DIM * q : DIM * q + DIM].bitcast(F32).rearrange("p (g r u) -> p g r u", g=PASSES, u=2)
+            engine(out=dst, in_=s.pop(("xt", j, q))[:].rearrange("p g u r -> p g r u"))
 
-        def quant_x(i):
-            if not ok(i):
-                return
-            xg = s.pop(("xg", i))
-            xc = work.tile([P, PASSES * P], U32, name="xc", align_bytes=64)
-            xs = work.tile([P, PASSES * P], U8, name="xs", align_bytes=64)
-            nc.vector.quantize_mx(out=xc[:].bitcast(FP8X4), scales=xs[:], in_=xg[:])
-            s["xq", i] = (xc, xs)
+        def quant_x(j):
+            n = span(j)
+            xc = work.tile([P, 2 * PASSES * P], U32, name="xc", align_bytes=64)
+            xs = work.tile([P, 2 * PASSES * P], U8, name="xs", align_bytes=64)
+            w = n * PASSES * P
+            nc.vector.quantize_mx(out=xc[:, 0:w].bitcast(FP8X4), scales=xs[:, 0:w], in_=s.pop(("xg", j))[:, 0 : 4 * w])
+            s["xq", j] = (xc, xs)
 
-        def x_passes(i, name, acc, last):
-            xc, xs = s["xq", i]
+        def x_passes(j, q, name, acc, last):
+            xc, xs = s["xq", j]
             for p in range(PASSES):
-                cols = slice(P * p, P * p + P)
+                cols = slice(P * (PASSES * q + p), P * (PASSES * q + p) + P)
                 nc.tensor.matmul_mx(
                     out=acc[:],
                     lhsT=xc[:, cols].bitcast(FP8X4),
@@ -202,139 +220,135 @@ def tile_softresidualsemanticids_d1p_kernel(
                     stop=(last and p == PASSES - 1),
                 )
 
-        def score1(i):
-            if not ok(i):
-                return
+        def score1(j, q):
             acc = psum.tile([P, CODES], F32, name="acc1")
-            x_passes(i, "c1", acc, True)
-            s["acc1", i] = acc
+            x_passes(j, q, "c1", acc, True)
+            s["acc1", j, q] = acc
 
-        def score2(i):
-            if not ok(i):
-                return
+        def score2(j, q):
             acc = psum.tile([P, CODES], F32, name="acc2")
-            x_passes(i, "c2", acc, False)
-            s["acc2", i] = acc
+            x_passes(j, q, "c2", acc, False)
+            s["acc2", j, q] = acc
 
-        def recon(i):
-            if not ok(i):
-                return
-            ac, as_ = s.pop(("aq", i))
+        def recon(j, q):
+            ac, as_ = s["aq", j]
+            cols = slice(P * q, P * q + P)
             nc.tensor.matmul_mx(
-                out=s["acc2", i][:],
-                lhsT=ac[:].bitcast(FP8X4),
-                lhsT_scale=as_[:],
+                out=s["acc2", j, q][:],
+                lhsT=ac[:, cols].bitcast(FP8X4),
+                lhsT_scale=as_[:, cols],
                 rhs=cross_codes[:].bitcast(FP8X4),
                 rhs_scale=cross_scales[:],
                 start=False,
                 stop=True,
             )
 
-        def logits1(i):
-            if not ok(i):
-                return
-            z = work.tile([P, CODES], F32, name="z")
+        def logits1(j, q):
+            if q == 0:
+                s["z", j] = work.tile([P, 2, CODES], F32, name="z")
             nc.vector.scalar_tensor_tensor(
-                out=z[:], in0=s.pop(("acc1", i))[:], scalar=-2.0, in1=row_b1[:], op0=ALU.mult, op1=ALU.subtract
+                out=s["z", j][:, q, :], in0=s.pop(("acc1", j, q))[:], scalar=-2.0, in1=row_b1[:],
+                op0=ALU.mult, op1=ALU.subtract,
             )
-            s["z", i] = z
 
-        def min1(i):
-            if not ok(i):
-                return
-            m = work.tile([P, 1], F32, name="m1")
-            nc.vector.tensor_reduce(out=m[:], in_=s["z", i][:], axis=AX.X, op=ALU.min)
-            s["m1", i] = m
+        def min1(j):
+            n = span(j)
+            m = work.tile([P, 2], F32, name="m1")
+            nc.vector.tensor_reduce(out=m[:, 0:n], in_=s["z", j][:, 0:n, :], axis=AX.X, op=ALU.min)
+            s["m1", j] = m
 
-        def exp1(i):
-            if not ok(i):
-                return
-            e = work.tile([P, CODES], F32, name="e")
-            total = work.tile([P, 1], F32, name="total")
+        def exp1(j, q):
+            if q == 0:
+                s["e", j] = work.tile([P, 2, CODES], F32, name="e")
+                s["total", j] = work.tile([P, 2], F32, name="total")
             nc.scalar.activation(
-                out=e[:], in_=s.pop(("z", i))[:], func=ACT.Exp, bias=s.pop(("m1", i))[:], scale=-1.0, accum_out=total[:]
+                out=s["e", j][:, q, :], in_=s["z", j][:, q, :], func=ACT.Exp, bias=s["m1", j][:, q : q + 1], scale=-1.0,
+                accum_out=s["total", j][:, q : q + 1],
             )
-            s["e", i] = e
-            s["total", i] = total
 
-        def recip1(i):
-            if not ok(i):
-                return
-            r = work.tile([P, 1], F32, name="r")
-            nc.vector.reciprocal(out=r[:], in_=s.pop(("total", i))[:])
-            s["r", i] = r
+        def recip1(j):
+            n = span(j)
+            r = work.tile([P, 2], F32, name="r")
+            nc.vector.reciprocal(out=r[:, 0:n], in_=s["total", j][:, 0:n])
+            s["r", j] = r
 
-        def amplitude(i):
-            if not ok(i):
+        def gain(j, q):
+            if AMP[GROUPS[j][0] + q] == "v":
                 return
-            a = work.tile([P, CODES], BF16, name="a")
+            eg = work.tile([P, CODES], F32, name="eg")
+            nc.gpsimd.tensor_tensor(out=eg[:], in0=s["e", j][:, q, :], in1=neg_g[:], op=ALU.mult)
+            s["eg", j, q] = eg
+
+        def amplitude(j, q):
+            if q == 0:
+                s["a", j] = work.tile([P, 2 * CODES], BF16, name="a")
+            how = AMP[GROUPS[j][0] + q]
+            if how != "v":
+                dst, eg, r = s["a", j][:, CODES * q : CODES * q + CODES], s.pop(("eg", j, q)), s["r", j][:, q : q + 1]
+                if how == "g":
+                    nc.vector.tensor_scalar(out=dst, in0=eg[:], scalar1=r, scalar2=None, op0=ALU.mult)
+                else:
+                    nc.scalar.activation(out=dst, in_=eg[:], func=ACT.Copy, scale=r)
+                return
             nc.vector.scalar_tensor_tensor(
-                out=a[:], in0=s.pop(("e", i))[:], scalar=s.pop(("r", i))[:], in1=neg_g[:], op0=ALU.mult, op1=ALU.mult
+                out=s["a", j][:, CODES * q : CODES * q + CODES], in0=s["e", j][:, q, :], scalar=s["r", j][:, q : q + 1],
+                in1=neg_g[:], op0=ALU.mult, op1=ALU.mult,
             )
-            s["a", i] = a
 
-        def turn_a(i):
-            if not ok(i):
-                return
-            w = s.pop(("a", i))[:].bitcast(F32)
-            at = psum.tile([P, 2, P], F32, name="at")
-            for u in range(2):
-                nc.tensor.transpose(at[:, u, :], w[:, u:256:2], ident[:])
-            s["at", i] = at
+        def turn_a(j):
+            w = s.pop(("a", j))[:].bitcast(F32)
+            at = psum.tile([P, 2, 2, P], F32, name="at")
+            for q in range(span(j)):
+                for u in range(2):
+                    nc.tensor.transpose(at[:, q, u, :], w[:, 256 * q + u : 256 * q + 256 : 2], ident[:])
+            s["at", j] = at
 
-        def copy_a(i):
-            if not ok(i):
-                return
-            at = s.pop(("at", i))
-            ag = work.tile([P, P * 4], BF16, name="ag", align_bytes=64)
-            nc.scalar.copy(out=ag[:].bitcast(F32).rearrange("p (r u) -> p r u", u=2), in_=at[:].rearrange("p u r -> p r u"))
-            s["ag", i] = ag
+        def copy_a(j):
+            n = span(j)
+            at = s.pop(("at", j))
+            ag = work.tile([P, 2 * CODES], BF16, name="ag", align_bytes=64)
+            nc.scalar.copy(
+                out=ag[:, 0 : n * CODES].bitcast(F32).rearrange("p (q r u) -> p q r u", q=n, u=2),
+                in_=at[:, 0:n].rearrange("p q u r -> p q r u"),
+            )
+            s["ag", j] = ag
 
-        def quant_a(i):
-            if not ok(i):
-                return
-            ac = work.tile([P, P], U32, name="ac", align_bytes=64)
-            as_ = work.tile([P, P], U8, name="as_", align_bytes=64)
-            nc.vector.quantize_mx(out=ac[:].bitcast(FP8X4), scales=as_[:], in_=s.pop(("ag", i))[:])
-            s["aq", i] = (ac, as_)
+        def quant_a(j):
+            n = span(j)
+            ac = work.tile([P, 2 * P], U32, name="ac", align_bytes=64)
+            as_ = work.tile([P, 2 * P], U8, name="as_", align_bytes=64)
+            nc.vector.quantize_mx(
+                out=ac[:, 0 : n * P].bitcast(FP8X4), scales=as_[:, 0 : n * P], in_=s.pop(("ag", j))[:, 0 : n * CODES]
+            )
+            s["aq", j] = (ac, as_)
 
-        def logits2(i):
-            if not ok(i):
-                return
-            nl = keep.tile([P, CODES], F32, name="nl_" + str(i))
+        def logits2(j, q):
+            if q == 0:
+                s["nl", j] = keep.tile([P, 2, CODES], F32, name="nl_" + str(j))
+            nl = s["nl", j][:, q, :]
             nc.vector.scalar_tensor_tensor(
-                out=nl[:], in0=s.pop(("acc2", i))[:], scalar=-1.0, in1=row_b2[:], op0=ALU.mult, op1=ALU.subtract
+                out=nl, in0=s.pop(("acc2", j, q))[:], scalar=-1.0, in1=row_b2[:], op0=ALU.mult, op1=ALU.subtract
             )
-            s["nl", i] = nl
+            s["nl1", GROUPS[j][0] + q] = nl
 
-        def min2_of(i):
-            if not ok(i):
-                return
-            nc.vector.tensor_reduce(out=min2[:, i : i + 1], in_=s["nl", i][:], axis=AX.X, op=ALU.min)
+        def min2_of(j):
+            lo, hi = GROUPS[j]
+            nc.vector.tensor_reduce(out=min2[:, lo:hi], in_=s["nl", j][:, 0 : hi - lo, :], axis=AX.X, op=ALU.min)
 
-        def exp2(i):
-            if not ok(i):
-                return
-            if i - LOG_WAIT + 1 in LOG_BATCHES:
-                series_end(LOG_BATCHES[i - LOG_WAIT + 1], i - LOG_WAIT + 1)
+        def exp2(j, q):
+            i = GROUPS[j][0] + q
+            if q == 0 and pending and j >= pending[0][0]:
+                series_end(*pending.pop(0)[1:])
             spill = work.tile([P, CODES], BF16, name="spill")
             nc.scalar.activation(
-                out=spill[:], in_=s["nl", i][:], func=ACT.Exp, bias=min2[:, i : i + 1], scale=-1.0,
+                out=spill[:], in_=s["nl1", i], func=ACT.Exp, bias=min2[:, i : i + 1], scale=-1.0,
                 accum_out=sum2[:, i : i + 1],
             )
-            if i + 1 in LOG_BATCHES:
-                lo = LOG_BATCHES[i + 1]
-                if i + 1 == TILES:
-                    last_logs(lo, i + 1)
-                else:
-                    series_start(lo, i + 1)
-
-        def last_logs(lo, hi):
-            logs = keep.tile([P, hi - lo], F32, name="logs")
-            shift = keep.tile([P, hi - lo], F32, name="shift_" + str(lo))
-            nc.scalar.activation(out=logs[:], in_=sum2[:, lo:hi], func=ACT.Ln, scale=1.0 / CODES)
-            nc.vector.tensor_tensor(out=shift[:], in0=min2[:, lo:hi], in1=logs[:], op=ALU.subtract)
-            finish(lo, hi, shift)
+            if i + 1 == TILES:
+                logs_of(LOG_BATCHES[i + 1], i + 1)
+            elif i + 1 in LOG_BATCHES:
+                series_start(LOG_BATCHES[i + 1], i + 1)
+                pending.append((j + LOG_WAIT, LOG_BATCHES[i + 1], i + 1))
 
         def series_start(lo, hi):
             n = hi - lo
@@ -371,17 +385,45 @@ def tile_softresidualsemanticids_d1p_kernel(
             nc.gpsimd.tensor_tensor(out=shift[:], in0=min2[:, lo:hi], in1=log[:], op=ALU.subtract)
             finish(lo, hi, shift)
 
+        def logs_of(lo, hi):
+            logs = keep.tile([P, hi - lo], F32, name="logs")
+            shift = keep.tile([P, hi - lo], F32, name="shift_" + str(lo))
+            nc.scalar.activation(out=logs[:], in_=sum2[:, lo:hi], func=ACT.Ln, scale=1.0 / CODES)
+            if hi == TILES:
+                finish_all()
+            nc.vector.tensor_tensor(out=shift[:], in0=min2[:, lo:hi], in1=logs[:], op=ALU.subtract)
+            finish(lo, hi, shift)
+            if hi == TILES:
+                finish_all()
+
         def finish(lo, hi, shift):
-            res = work.tile([P, 6, CODES], F32, name="res", bufs=2)
-            for i in range(lo, hi):
-                who = FINISH[i]
-                src, dst, sh = s.pop(("nl", i))[:], res[:, i - lo, :], shift[:, i - lo : i - lo + 1]
-                if who == "s":
-                    nc.scalar.activation(out=dst, in_=src, func=ACT.Identity, bias=sh, scale=-1.0)
-                else:
-                    eng = nc.vector if who == "v" else nc.gpsimd
-                    eng.tensor_scalar(out=dst, in0=src, scalar1=-1.0, scalar2=sh, op0=ALU.mult, op1=ALU.add)
-            nc.sync.dma_start(out=out_view[:, lo:hi, :], in_=res[:, 0 : hi - lo, :])
+            size = 1 if hi == TILES else STORE
+            for a in range(lo, hi, size):
+                b = min(a + size, hi)
+                for i in range(a, b):
+                    todo.append((i, a, b, shift[:, i - lo : i - lo + 1], s["step"] + FIN_WAIT))
+
+        def finish_all():
+            while todo:
+                finish_one()
+
+        todo = []
+        pending = []
+
+        def finish_one():
+            i, a, b, sh, ready = todo.pop(0)
+            if i == a:
+                res = work.tile([P, STORE, CODES], F32, name="res", bufs=6)
+                s["res"] = res
+            dst = s["res"][:, i - a, :]
+            src = s.pop(("nl1", i))
+            if FINISH[i] == "s":
+                nc.scalar.activation(out=dst, in_=src, func=ACT.Identity, bias=sh, scale=-1.0)
+            else:
+                eng = nc.vector if FINISH[i] == "v" else nc.gpsimd
+                eng.tensor_scalar(out=dst, in0=src, scalar1=-1.0, scalar2=sh, op0=ALU.mult, op1=ALU.add)
+            if i == b - 1:
+                nc.sync.dma_start(out=out_view[:, a:b, :], in_=s["res"][:, 0 : b - a, :])
 
         cross_rows = keep.tile([P, 4, CODES], BF16, name="cross_rows")
         cross_grouped = keep.tile([P, 4 * CODES], BF16, name="cross_grouped", align_bytes=64)
@@ -443,12 +485,20 @@ def tile_softresidualsemanticids_d1p_kernel(
         pieces = {1: cross_1, 2: cross_2, 3: cross_3, 4: cross_4, 5: cross_quant}
         ops = {
             "widen": widen, "turn_x": turn_x, "copy_x": copy_x, "quant_x": quant_x, "score1": score1,
-            "logits1": logits1, "min1": min1, "exp1": exp1, "recip1": recip1, "amplitude": amplitude,
+            "logits1": logits1, "min1": min1, "exp1": exp1, "recip1": recip1, "amplitude": amplitude, "gain": gain,
             "turn_a": turn_a, "copy_a": copy_a, "quant_a": quant_a, "score2": score2, "recon": recon,
             "logits2": logits2, "min2": min2_of, "exp2": exp2,
         }
-        for k in range(-4, TILES + 6):
-            for name, lag in STEP:
-                ops[name](k - lag)
-                for piece in CROSS.get((k, name), ()):
+        for k in range(-6, len(GROUPS) + 7):
+            s["step"] = k
+            for name, lag, q in STEP:
+                if name == "finish":
+                    if k >= lag and todo and k >= todo[0][4]:
+                        finish_one()
+                elif ok(k - lag):
+                    if q < 0:
+                        ops[name](k - lag)
+                    elif q < span(k - lag):
+                        ops[name](k - lag, q)
+                for piece in CROSS.get((k, name, q), ()):
                     pieces[piece]()

import math
from contextlib import ExitStack

import concourse.mybir as mybir
from concourse.masks import make_identity

TOKENS, DIM, CODES = 2048, 1024, 512
FLOPS = 2 * (2 * TOKENS * DIM * CODES + CODES * DIM * CODES + TOKENS * CODES * CODES)

F32 = mybir.dt.float32
BF16 = mybir.dt.bfloat16
I32 = mybir.dt.int32
U32 = mybir.dt.uint32
U8 = mybir.dt.uint8
FP8 = mybir.dt.float8_e4m3fn
FP8X4 = mybir.dt.float8_e4m3fn_x4
FP4X4 = mybir.dt.float4_e2m1fn_x4
ALU = mybir.AluOpType
ACT = mybir.ActivationFunctionType
AX = mybir.AxisListType

P = 128
TILES = TOKENS // P
PASSES = DIM // 512
BLOCKS = DIM // 128
CHUNKS = [(0, 1), (1, 3), (3, 6), (6, 10), (10, 14), (14, 16)]
LOG_BATCHES = {7: 0, 11: 7, 16: 11}
FINISH = "ssssvvvvvvvvvvvv"
VECTOR_BLOCKS = [2, 5, 0, 2, 1, 5, 2, 1, 2, 0, 2, 0, 2, 0, 0, 0]
VECTOR_COPIES = [0, 1]
STORE = 1
ROOT = 256.0
LOG_WAIT = 1
FIN_WAIT = 2
AMP = "vvvvvvvvvvvvvvvv"
CROSS_OUT = "vvss"
CROSS_COPY = "vv"
GROUPS = [(0, 1), (1, 3), (3, 5), (5, 7), (7, 9), (9, 11), (11, 13), (13, 15), (15, 16)]
STEP = (
    ("logits1", 0, 0),
    ("turn_x", -2, 0),
    ("widen", -3, 0),
    ("logits1", 0, 1),
    ("amplitude", 1, 0),
    ("amplitude", 1, 1),
    ("turn_x", -2, 1),
    ("finish", 1, 0),
    ("min1", 0, -1),
    ("exp2", 3, 0),
    ("logits2", 2, 0),
    ("quant_x", -1, -1),
    ("turn_a", 1, -1),
    ("exp2", 3, 1),
    ("copy_a", 1, -1),
    ("score2", 1, 0),
    ("logits2", 2, 1),
    ("score1", -1, 0),
    ("exp1", 0, 0),
    ("score1", -1, 1),
    ("quant_a", 1, -1),
    ("recon", 1, 0),
    ("exp1", 0, 1),
    ("finish", -1, 2),
    ("min2", 2, -1),
    ("widen", -3, 1),
    ("copy_x", -2, 0),
    ("finish", 27, 1),
    ("score2", 1, 1),
    ("recip1", 0, -1),
    ("copy_x", -2, 1),
    ("finish", -15, 3),
    ("recon", 1, 1),
)
CROSS = {(-1, "widen", 0): (1,), (-1, "finish", 2): (2,), (0, "turn_x", 0): (3,), (0, "copy_a", -1): (4,), (1, "copy_a", -1): (5,)}


def tile_softresidualsemanticids_d1p_kernel(
    tc, x_bytes, x_scale, c1_words, c1_scales, v1_words, v1_scales, c2_words, c2_scales, g, b1, b2, out
):
    nc = tc.nc
    x_view = x_bytes.rearrange("(p i) k -> p i k", i=TILES)
    out_view = out.rearrange("(p i) m -> p i m", i=TILES)

    with ExitStack() as ctx:
        keep = ctx.enter_context(tc.tile_pool(name="keep", bufs=1))
        work = ctx.enter_context(tc.tile_pool(name="work", bufs=3))
        psum = ctx.enter_context(tc.psum_pool(name="psum", bufs=2))
        ctx.enter_context(tc.manual_schedule())

        scale_planes = {}
        for name in ("c1", "v1", "c2"):
            plane = keep.tile([P, PASSES, CODES], U8, name="scales_" + name, align_bytes=64)
            nc.vector.memset(plane[:].rearrange("p g n -> p (g n)").bitcast(I32), 0)
            scale_planes[name] = plane
        ident = keep.tile([P, P], F32, name="ident")
        make_identity(nc, ident[:])

        words = {}

        def load_words(name, source, queue=nc.gpsimd):
            tile = keep.tile([P, PASSES, 2 * CODES], U8, name="words_" + name, align_bytes=64)
            queue.dma_start(
                out=tile[:].rearrange("p g n -> p (g n)").bitcast(I32).rearrange("p (g n) -> p g n", g=PASSES),
                in_=source.bitcast(I32).rearrange("g p n -> p g n"),
            )
            words[name] = tile

        def load_scales(name, source):
            plane = scale_planes[name]
            view = plane[:].rearrange("p g n -> p (g n)").bitcast(I32).rearrange("p (g n) -> p g n", g=PASSES)
            rows = source.bitcast(I32).rearrange("g q n -> q g n")
            for quad in range(4):
                nc.sync.dma_start(out=view[32 * quad : 32 * quad + 4], in_=rows[4 * quad : 4 * quad + 4])

        def load_row(name, source, queue=nc.gpsimd):
            tile = keep.tile([P, CODES], BF16, name="row_" + name)
            queue.dma_start(out=tile[:], in_=source.partition_broadcast(P))
            return tile

        x_tiles = {}

        def load_x(chunk):
            lo, hi = chunk
            tile = keep.tile([P, hi - lo, DIM], U8, name="xbytes_" + str(lo), align_bytes=64)
            nc.sync.dma_start(out=tile[:], in_=x_view[:, lo:hi, :])
            for i in range(lo, hi):
                x_tiles[i] = (tile, i - lo)

        load_x(CHUNKS[0])
        scale_cols = keep.tile([P, TILES * BLOCKS], F32, name="scale_cols")
        nc.sync.dma_start(out=scale_cols[:], in_=x_scale.rearrange("(p i) j -> p (i j)", i=TILES))
        load_scales("c1", c1_scales)
        load_words("c1", c1_words, nc.sync)
        load_x(CHUNKS[1])
        row_b1 = load_row("b1", b1, nc.sync)
        load_words("v1", v1_words)
        load_words("c2", c2_words)
        row_g = load_row("g", g)
        row_b2 = load_row("b2", b2)
        neg_g = keep.tile([P, CODES], BF16, name="neg_g")
        nc.gpsimd.tensor_scalar(out=neg_g[:], in0=row_g[:], scalar1=-1.0, scalar2=0.0, op0=ALU.mult, op1=ALU.add)
        load_scales("v1", v1_scales)
        load_scales("c2", c2_scales)
        for chunk in CHUNKS[2:]:
            load_x(chunk)
        warm = keep.tile([P, 1], F32, name="warm")
        nc.vector.memset(warm[:], 0.0)
        warm_out = keep.tile([P, 1], F32, name="warm_out")
        nc.scalar.activation(out=warm_out[:], in_=warm[:], func=ACT.Exp)

        root = keep.tile([P, 2, TILES], F32, name="root")
        nc.gpsimd.memset(root[:, 0, :], 1.0 / ROOT)
        nc.gpsimd.memset(root[:, 1, :], -1.0 / ROOT)

        s = {}
        min2 = keep.tile([P, TILES], F32, name="min2")
        sum2 = keep.tile([P, TILES], F32, name="sum2")

        def mover(who):
            return nc.vector.tensor_copy if who == "v" else nc.scalar.copy

        def ok(j):
            return 0 <= j < len(GROUPS)

        def tiles(j):
            return range(GROUPS[j][0], GROUPS[j][1])

        def span(j):
            return GROUPS[j][1] - GROUPS[j][0]

        def widen(j, q):
            if q == 0:
                s["xb", j] = work.tile([P, 2, DIM], BF16, name="xb")
            i = GROUPS[j][0] + q
            tile, slot = x_tiles[i]
            xb = s["xb", j]
            for b in range(BLOCKS):
                cols = slice(128 * b, 128 * b + 128)
                src = tile[:, slot, cols].bitcast(FP8)
                scale = scale_cols[:, BLOCKS * i + b : BLOCKS * i + b + 1]
                if b < VECTOR_BLOCKS[i]:
                    nc.vector.tensor_scalar(out=xb[:, q, cols], in0=src, scalar1=scale, scalar2=None, op0=ALU.mult)
                else:
                    nc.scalar.activation(out=xb[:, q, cols], in_=src, func=ACT.Copy, scale=scale)

        def turn_x(j, q):
            w = s["xb", j][:, q, :].bitcast(F32)
            xt = psum.tile([P, PASSES, 2, P], F32, name="xt")
            for p in range(PASSES):
                for u in range(2):
                    nc.tensor.transpose(xt[:, p, u, :], w[:, 256 * p + u : 256 * (p + 1) : 2], ident[:])
            s["xt", j, q] = xt

        def copy_x(j, q):
            if q == 0:
                s["xg", j] = work.tile([P, 2 * PASSES * P * 4], BF16, name="xg", align_bytes=64)
            engine = nc.vector.tensor_copy if GROUPS[j][0] + q in VECTOR_COPIES else nc.scalar.copy
            dst = s["xg", j][:, DIM * q : DIM * q + DIM].bitcast(F32).rearrange("p (g r u) -> p g r u", g=PASSES, u=2)
            engine(out=dst, in_=s.pop(("xt", j, q))[:].rearrange("p g u r -> p g r u"))

        def quant_x(j):
            n = span(j)
            xc = work.tile([P, 2 * PASSES * P], U32, name="xc", align_bytes=64)
            xs = work.tile([P, 2 * PASSES * P], U8, name="xs", align_bytes=64)
            w = n * PASSES * P
            nc.vector.quantize_mx(out=xc[:, 0:w].bitcast(FP8X4), scales=xs[:, 0:w], in_=s.pop(("xg", j))[:, 0 : 4 * w])
            s["xq", j] = (xc, xs)

        def x_passes(j, q, name, acc, last):
            xc, xs = s["xq", j]
            for p in range(PASSES):
                cols = slice(P * (PASSES * q + p), P * (PASSES * q + p) + P)
                nc.tensor.matmul_mx(
                    out=acc[:],
                    lhsT=xc[:, cols].bitcast(FP8X4),
                    lhsT_scale=xs[:, cols],
                    rhs=words[name][:, p, :].bitcast(FP4X4),
                    rhs_scale=scale_planes[name][:, p, :],
                    start=(p == 0),
                    stop=(last and p == PASSES - 1),
                )

        def score1(j, q):
            acc = psum.tile([P, CODES], F32, name="acc1")
            x_passes(j, q, "c1", acc, True)
            s["acc1", j, q] = acc

        def score2(j, q):
            acc = psum.tile([P, CODES], F32, name="acc2")
            x_passes(j, q, "c2", acc, False)
            s["acc2", j, q] = acc

        def recon(j, q):
            ac, as_ = s["aq", j]
            cols = slice(P * q, P * q + P)
            nc.tensor.matmul_mx(
                out=s["acc2", j, q][:],
                lhsT=ac[:, cols].bitcast(FP8X4),
                lhsT_scale=as_[:, cols],
                rhs=cross_codes[:].bitcast(FP8X4),
                rhs_scale=cross_scales[:],
                start=False,
                stop=True,
            )

        def logits1(j, q):
            if q == 0:
                s["z", j] = work.tile([P, 2, CODES], F32, name="z")
            nc.vector.scalar_tensor_tensor(
                out=s["z", j][:, q, :], in0=s.pop(("acc1", j, q))[:], scalar=-2.0, in1=row_b1[:],
                op0=ALU.mult, op1=ALU.subtract,
            )

        def min1(j):
            n = span(j)
            m = work.tile([P, 2], F32, name="m1")
            nc.vector.tensor_reduce(out=m[:, 0:n], in_=s["z", j][:, 0:n, :], axis=AX.X, op=ALU.min)
            s["m1", j] = m

        def exp1(j, q):
            if q == 0:
                s["e", j] = work.tile([P, 2, CODES], F32, name="e")
                s["total", j] = work.tile([P, 2], F32, name="total")
            nc.scalar.activation(
                out=s["e", j][:, q, :], in_=s["z", j][:, q, :], func=ACT.Exp, bias=s["m1", j][:, q : q + 1], scale=-1.0,
                accum_out=s["total", j][:, q : q + 1],
            )

        def recip1(j):
            n = span(j)
            r = work.tile([P, 2], F32, name="r")
            nc.vector.reciprocal(out=r[:, 0:n], in_=s["total", j][:, 0:n])
            s["r", j] = r

        def gain(j, q):
            if AMP[GROUPS[j][0] + q] == "v":
                return
            eg = work.tile([P, CODES], F32, name="eg")
            nc.gpsimd.tensor_tensor(out=eg[:], in0=s["e", j][:, q, :], in1=neg_g[:], op=ALU.mult)
            s["eg", j, q] = eg

        def amplitude(j, q):
            if q == 0:
                s["a", j] = work.tile([P, 2 * CODES], BF16, name="a")
            how = AMP[GROUPS[j][0] + q]
            if how != "v":
                dst, eg, r = s["a", j][:, CODES * q : CODES * q + CODES], s.pop(("eg", j, q)), s["r", j][:, q : q + 1]
                if how == "g":
                    nc.vector.tensor_scalar(out=dst, in0=eg[:], scalar1=r, scalar2=None, op0=ALU.mult)
                else:
                    nc.scalar.activation(out=dst, in_=eg[:], func=ACT.Copy, scale=r)
                return
            nc.vector.scalar_tensor_tensor(
                out=s["a", j][:, CODES * q : CODES * q + CODES], in0=s["e", j][:, q, :], scalar=s["r", j][:, q : q + 1],
                in1=neg_g[:], op0=ALU.mult, op1=ALU.mult,
            )

        def turn_a(j):
            w = s.pop(("a", j))[:].bitcast(F32)
            at = psum.tile([P, 2, 2, P], F32, name="at")
            for q in range(span(j)):
                for u in range(2):
                    nc.tensor.transpose(at[:, q, u, :], w[:, 256 * q + u : 256 * q + 256 : 2], ident[:])
            s["at", j] = at

        def copy_a(j):
            n = span(j)
            at = s.pop(("at", j))
            ag = work.tile([P, 2 * CODES], BF16, name="ag", align_bytes=64)
            nc.scalar.copy(
                out=ag[:, 0 : n * CODES].bitcast(F32).rearrange("p (q r u) -> p q r u", q=n, u=2),
                in_=at[:, 0:n].rearrange("p q u r -> p q r u"),
            )
            s["ag", j] = ag

        def quant_a(j):
            n = span(j)
            ac = work.tile([P, 2 * P], U32, name="ac", align_bytes=64)
            as_ = work.tile([P, 2 * P], U8, name="as_", align_bytes=64)
            nc.vector.quantize_mx(
                out=ac[:, 0 : n * P].bitcast(FP8X4), scales=as_[:, 0 : n * P], in_=s.pop(("ag", j))[:, 0 : n * CODES]
            )
            s["aq", j] = (ac, as_)

        def logits2(j, q):
            if q == 0:
                s["nl", j] = keep.tile([P, 2, CODES], F32, name="nl_" + str(j))
            nl = s["nl", j][:, q, :]
            nc.vector.scalar_tensor_tensor(
                out=nl, in0=s.pop(("acc2", j, q))[:], scalar=-1.0, in1=row_b2[:], op0=ALU.mult, op1=ALU.subtract
            )
            s["nl1", GROUPS[j][0] + q] = nl

        def min2_of(j):
            lo, hi = GROUPS[j]
            nc.vector.tensor_reduce(out=min2[:, lo:hi], in_=s["nl", j][:, 0 : hi - lo, :], axis=AX.X, op=ALU.min)

        def exp2(j, q):
            i = GROUPS[j][0] + q
            if q == 0 and pending and j >= pending[0][0]:
                series_end(*pending.pop(0)[1:])
            spill = work.tile([P, CODES], BF16, name="spill")
            nc.scalar.activation(
                out=spill[:], in_=s["nl1", i], func=ACT.Exp, bias=min2[:, i : i + 1], scale=-1.0,
                accum_out=sum2[:, i : i + 1],
            )
            if i + 1 == TILES:
                logs_of(LOG_BATCHES[i + 1], i + 1)
            elif i + 1 in LOG_BATCHES:
                series_start(LOG_BATCHES[i + 1], i + 1)
                pending.append((j + LOG_WAIT, LOG_BATCHES[i + 1], i + 1))

        def series_start(lo, hi):
            n = hi - lo
            total = sum2[:, lo:hi]
            up = work.tile([P, n], F32, name="up")
            nc.gpsimd.tensor_tensor(out=up[:], in0=total, in1=root[:, 0, 0:n], op=ALU.pow)
            down = work.tile([P, n], F32, name="down")
            nc.gpsimd.tensor_tensor(out=down[:], in0=total, in1=root[:, 1, 0:n], op=ALU.pow)
            sinh2 = work.tile([P, n], F32, name="sinh2")
            nc.gpsimd.tensor_tensor(out=sinh2[:], in0=up[:], in1=down[:], op=ALU.subtract)
            s["log", lo] = sinh2

        def series_end(lo, hi):
            n = hi - lo
            total = sum2[:, lo:hi]
            sinh2 = s.pop(("log", lo))
            shift = keep.tile([P, n], F32, name="shift_" + str(lo))
            inv = work.tile([P, n], F32, name="inv")
            nc.scalar.activation(out=inv[:], in_=sinh2[:], func=ACT.Exp, scale=-0.5 * ROOT)
            ratio = work.tile([P, n], F32, name="ratio")
            nc.gpsimd.tensor_tensor(out=ratio[:], in0=total, in1=inv[:], op=ALU.mult)
            guess = work.tile([P, n], F32, name="guess")
            nc.gpsimd.tensor_scalar(
                out=guess[:], in0=sinh2[:], scalar1=0.5 * ROOT, scalar2=-math.log(CODES), op0=ALU.mult, op1=ALU.add
            )
            delta = work.tile([P, n], F32, name="delta")
            nc.gpsimd.tensor_scalar(out=delta[:], in0=ratio[:], scalar1=1.0, scalar2=-1.0, op0=ALU.mult, op1=ALU.add)
            slope = work.tile([P, n], F32, name="slope")
            nc.gpsimd.tensor_scalar(out=slope[:], in0=ratio[:], scalar1=-0.5, scalar2=1.5, op0=ALU.mult, op1=ALU.add)
            prod = work.tile([P, n], F32, name="prod")
            nc.gpsimd.tensor_tensor(out=prod[:], in0=slope[:], in1=delta[:], op=ALU.mult)
            log = work.tile([P, n], F32, name="log")
            nc.gpsimd.tensor_tensor(out=log[:], in0=prod[:], in1=guess[:], op=ALU.add)
            nc.gpsimd.tensor_tensor(out=shift[:], in0=min2[:, lo:hi], in1=log[:], op=ALU.subtract)
            finish(lo, hi, shift)

        def logs_of(lo, hi):
            logs = keep.tile([P, hi - lo], F32, name="logs")
            shift = keep.tile([P, hi - lo], F32, name="shift_" + str(lo))
            nc.scalar.activation(out=logs[:], in_=sum2[:, lo:hi], func=ACT.Ln, scale=1.0 / CODES)
            if hi == TILES:
                finish_all()
            nc.vector.tensor_tensor(out=shift[:], in0=min2[:, lo:hi], in1=logs[:], op=ALU.subtract)
            finish(lo, hi, shift)
            if hi == TILES:
                finish_all()

        def finish(lo, hi, shift):
            size = 1 if hi == TILES else STORE
            for a in range(lo, hi, size):
                b = min(a + size, hi)
                for i in range(a, b):
                    todo.append((i, a, b, shift[:, i - lo : i - lo + 1], s["step"] + FIN_WAIT))

        def finish_all():
            while todo:
                finish_one()

        todo = []
        pending = []

        def finish_one():
            i, a, b, sh, ready = todo.pop(0)
            if i == a:
                res = work.tile([P, STORE, CODES], F32, name="res", bufs=6)
                s["res"] = res
            dst = s["res"][:, i - a, :]
            src = s.pop(("nl1", i))
            if FINISH[i] == "s":
                nc.scalar.activation(out=dst, in_=src, func=ACT.Identity, bias=sh, scale=-1.0)
            else:
                eng = nc.vector if FINISH[i] == "v" else nc.gpsimd
                eng.tensor_scalar(out=dst, in0=src, scalar1=-1.0, scalar2=sh, op0=ALU.mult, op1=ALU.add)
            if i == b - 1:
                nc.sync.dma_start(out=out_view[:, a:b, :], in_=s["res"][:, 0 : b - a, :])

        cross_rows = keep.tile([P, 4, CODES], BF16, name="cross_rows")
        cross_grouped = keep.tile([P, 4 * CODES], BF16, name="cross_grouped", align_bytes=64)
        cross_codes = keep.tile([P, CODES], U32, name="cross_codes", align_bytes=64)
        cross_scales = keep.tile([P, CODES], U8, name="cross_scales", align_bytes=64)

        def cross_mm(j):
            acc = psum.tile([P, CODES], F32, name="acc2")
            for p in range(PASSES):
                nc.tensor.matmul_mx(
                    out=acc[:],
                    lhsT=words["c2"][:, p, 256 * j : 256 * j + 256].bitcast(FP4X4),
                    lhsT_scale=scale_planes["c2"][:, p, P * j : P * j + P],
                    rhs=words["v1"][:, p, :].bitcast(FP4X4),
                    rhs_scale=scale_planes["v1"][:, p, :],
                    start=(p == 0),
                    stop=(p == PASSES - 1),
                )
            s["cross", j] = acc

        def cross_out(j, engine):
            engine(out=cross_rows[:, j, :], in_=s.pop(("cross", j))[:])

        def cross_turn(h):
            ct = psum.tile([P, 2, 2, P], F32, name="at")
            for jj in range(2):
                w = cross_rows[:, 2 * h + jj, :].bitcast(F32)
                for u in range(2):
                    nc.tensor.transpose(ct[:, jj, u, :], w[:, u:256:2], ident[:])
            s["ct", h] = ct

        def cross_copy(h, engine):
            dst = cross_grouped[:].bitcast(F32).rearrange("p (h j m u) -> p h j m u", h=2, j=2, u=2)[:, h]
            engine(out=dst, in_=s.pop(("ct", h))[:].rearrange("p j u m -> p j m u"))

        def cross_quant():
            nc.vector.quantize_mx(out=cross_codes[:].bitcast(FP8X4), scales=cross_scales[:], in_=cross_grouped[:])

        def cross_1():
            cross_mm(0)
            cross_mm(1)

        def cross_2():
            cross_out(0, mover(CROSS_OUT[0]))
            cross_out(1, mover(CROSS_OUT[1]))
            cross_mm(2)
            cross_mm(3)

        def cross_3():
            cross_out(2, mover(CROSS_OUT[2]))
            cross_out(3, mover(CROSS_OUT[3]))
            cross_turn(0)
            cross_turn(1)

        def cross_4():
            cross_copy(0, mover(CROSS_COPY[0]))
            cross_copy(1, mover(CROSS_COPY[1]))

        pieces = {1: cross_1, 2: cross_2, 3: cross_3, 4: cross_4, 5: cross_quant}
        ops = {
            "widen": widen, "turn_x": turn_x, "copy_x": copy_x, "quant_x": quant_x, "score1": score1,
            "logits1": logits1, "min1": min1, "exp1": exp1, "recip1": recip1, "amplitude": amplitude, "gain": gain,
            "turn_a": turn_a, "copy_a": copy_a, "quant_a": quant_a, "score2": score2, "recon": recon,
            "logits2": logits2, "min2": min2_of, "exp2": exp2,
        }
        for k in range(-6, len(GROUPS) + 7):
            s["step"] = k
            for name, lag, q in STEP:
                if name == "finish":
                    if k >= lag and todo and k >= todo[0][4]:
                        finish_one()
                elif ok(k - lag):
                    if q < 0:
                        ops[name](k - lag)
                    elif q < span(k - lag):
                        ops[name](k - lag, q)
                for piece in CROSS.get((k, name, q), ()):
                    pieces[piece]()
